import numpy as np
import ml_dtypes


def mxq(x, axis, fmt="e4m3"):
    dtype, down = {"e4m3": (ml_dtypes.float8_e4m3fn, 7), "e5m2": (ml_dtypes.float8_e5m2, 14)}[fmt]
    v = np.moveaxis(np.asarray(x, np.float32).astype(ml_dtypes.bfloat16).astype(np.float64), axis, -1)
    blocks = v.reshape(v.shape[:-1] + (-1, 32))
    amax = np.abs(blocks).max(-1, keepdims=True)
    byte = np.maximum(np.where(amax > 0, np.frexp(amax)[1] - 1 + 127, 0) - down, 1)
    scale = np.exp2(byte - 127.0)
    codes = (blocks / scale).astype(np.float32).astype(dtype).astype(np.float64)
    return np.moveaxis((codes * scale).reshape(v.shape), -1, axis)


WIDE = False


def mx_kscale(k):
    if not WIDE:
        return np.ones(k)
    levels = np.array([30, -30])
    if k % 512:
        return np.exp2(np.random.permutation(np.resize(levels, k // 32))).repeat(32)
    a = np.empty((k // 512, 16))
    for p in range(k // 512):
        a[p, :8] = np.random.permutation(np.resize(levels, 8))
        for g in range(8):
            far = levels[np.abs(levels - a[p, g]) >= 10]
            a[p, g + 8] = far[np.random.randint(len(far))]
    return np.exp2(a.ravel()).repeat(32)


def f64(x):
    return np.asarray(x).astype(np.float64)


E2M1 = np.array([0.0, 0.5, 1.0, 1.5, 2.0, 3.0, 4.0, 6.0, -0.0, -0.5, -1.0, -1.5, -2.0, -3.0, -4.0, -6.0])


def pack_weight(w, fmt):
    k, n = w.shape
    w = f64(np.asarray(w, np.float32).astype(ml_dtypes.bfloat16)).reshape(k // 32, 32, n)
    amax = np.abs(w).max(1)
    if fmt == "e4m3":
        byte = np.frexp(amax)[1] - 1 + 127 - 7
    else:
        mant, ex = np.frexp(amax / 6.0)
        byte = np.where(mant > 0.5, ex, ex - 1) + 127
    byte = np.clip(np.where(amax > 0, byte, 1), 1, 254)
    scaled = (w * np.exp2(127.0 - byte)[:, None, :]).reshape(k, n).astype(np.float32)
    by_word = np.ascontiguousarray(scaled.reshape(k // 512, 128, 4, n).transpose(0, 1, 3, 2))
    if fmt == "e4m3":
        words = by_word.astype(ml_dtypes.float8_e4m3fn).view(np.uint8)
    else:
        c = by_word.astype(ml_dtypes.float4_e2m1fn).view(np.uint8) & 0xF
        words = (c[..., 0::2] | (c[..., 1::2] << 4)).reshape(k // 512, 128, 2 * n)
    return np.ascontiguousarray(words), np.ascontiguousarray(byte.astype(np.uint8).reshape(k // 512, 16, n))


def unpack_weight(words, scales, fmt):
    g, _, n = scales.shape
    words = np.ascontiguousarray(words).reshape(g, 128, n, -1)
    if fmt == "e4m3":
        vals = words.view(ml_dtypes.float8_e4m3fn).astype(np.float64)
    else:
        nib = np.empty((g, 128, n, 4), np.uint8)
        nib[..., 0::2] = words & 0xF
        nib[..., 1::2] = words >> 4
        vals = E2M1[nib]
    vals = vals * np.repeat(np.exp2(scales.astype(np.float64) - 127.0), 8, axis=1)[..., None]
    return vals.transpose(0, 1, 3, 2).reshape(g * 512, n)


def bf(x):
    return np.asarray(x, np.float32).astype(ml_dtypes.bfloat16)


def planes(Y):
    r, m = Y.shape
    b = f64(bf(Y)).reshape(r // 32, 32, m)
    amax = np.abs(b).max(1)
    byte = np.clip(np.where(amax > 0, np.frexp(amax)[1] - 1 + 127 - 7, 1), 1, 254)
    codes = (b * np.exp2(127.0 - byte)[:, None, :]).reshape(r, m).astype(np.float32).astype(ml_dtypes.float8_e4m3fn).view(np.uint8)
    words = codes.reshape(r // 512, 128, 4, m).transpose(0, 1, 3, 2)
    return np.ascontiguousarray(words), np.ascontiguousarray(byte.astype(np.uint8).reshape(r // 512, 16, m))


N, R, K, T = 1024, 512, 512, 512


def setup_inputs():
    n = np.random.standard_normal
    fn = mx_kscale(N)
    fr = mx_kscale(R)
    wdp = pack_weight(n((N, R)) * 1 / np.sqrt(N) * fn[:, None], "e4m3")
    wap = pack_weight(n((R, K)) * 1 / np.sqrt(R) / fr[:, None], "e2m1")
    wbp = pack_weight(n((R, K)) * 1 / np.sqrt(R) / fr[:, None], "e4m3")
    return {
        "g": (n((N, T)) * np.exp(0.5 * n((1, T))) / fn[:, None]).astype(np.float32),
        "wd_words": wdp[0],
        "wd_scales": wdp[1],
        "gs": (np.random.uniform(0.05, 0.95, (R, T)) * fr[:, None]).astype(np.float32),
        "zs": (n((R, T)) * fr[:, None]).astype(np.float32),
        "wa_words": wap[0],
        "wa_scales": wap[1],
        "wb_words": wbp[0],
        "wb_scales": wbp[1],
    }


def reference(g, wd_words, wd_scales, gs, zs, wa_words, wa_scales, wb_words, wb_scales):
    wdu = unpack_weight(wd_words, wd_scales, "e4m3")
    wau = unpack_weight(wa_words, wa_scales, "e2m1")
    wbu = unpack_weight(wb_words, wb_scales, "e4m3")
    gq = mxq(f64(g), 0, "e5m2")
    d = wdu.T @ gq
    da = d * f64(gs)
    db = d * f64(zs)
    daq = mxq(da, 0, "e5m2")
    dbq = mxq(db, 0, "e4m3")
    y = wau.T @ daq + wbu.T @ dbq
    words, scales = planes(y)
    return y, words, scales

@@ -1,0 +1,278 @@
+from contextlib import ExitStack
+
+import concourse.mybir as mybir
+
+N, R, K, T = 1024, 512, 512, 512
+FLOPS = 2 * T * (N * R + 2 * R * K)
+
+F32 = mybir.dt.float32
+BF16 = mybir.dt.bfloat16
+I32 = mybir.dt.int32
+U8 = mybir.dt.uint8
+E4M3 = mybir.dt.float8_e4m3fn_x4
+E5M2 = mybir.dt.float8_e5m2_x4
+E2M1 = mybir.dt.float4_e2m1fn_x4
+MULT = mybir.AluOpType.mult
+
+P = 128
+PACK = 4
+HALF = T // 2
+QUARTER = T // 4
+WB_ROW = 4
+
+
+def tile_mix_gradient_of_gated_sum_pl_kernel(
+    tc, g, wd_words, wd_scales, gs, zs, wa_words, wa_scales, wb_words, wb_scales, out_0, out_1, out_2
+):
+    nc = tc.nc
+    passes = N // (P * PACK)
+
+    with ExitStack() as ctx:
+        sb = ctx.enter_context(tc.tile_pool(name="sb", bufs=1))
+        ps = ctx.enter_context(tc.psum_pool(name="ps", bufs=1))
+        ctx.enter_context(tc.manual_schedule())
+
+        def tile(name, shape, dtype):
+            return sb.tile(shape, dtype, name=name, align_bytes=64)
+
+        def rows_view(src, t0, width, run):
+            return src[:, :, t0 : t0 + width].rearrange("p j (c i) -> p c j i", i=run)
+
+        def word_view(dst, run):
+            return dst[:].rearrange("p (c i) j -> p c j i", i=run)
+
+        def quantize(codes, scales, t0, grouped, fmt):
+            width = grouped.shape[1]
+            nc.vector.quantize_mx(
+                out=codes[:, t0 : t0 + width].bitcast(fmt),
+                scales=scales[:, t0 : t0 + width],
+                in_=grouped[:].rearrange("p t j -> p (t j)"),
+            )
+
+        wd_scale_raw = tile("wd_scale_raw", [P, passes, R], U8)
+        ab_scale_raw = tile("ab_scale_raw", [P, K], U8)
+        nc.vector.memset(wd_scale_raw[:].bitcast(I32), 0)
+        nc.gpsimd.memset(ab_scale_raw[:].bitcast(I32), 0)
+
+        g_raw = [tile("g_raw%d" % z, [P, PACK, T], F32) for z in range(passes)]
+        wd_raw = tile("wd_raw", [P, passes, R], I32)
+        wa_raw = tile("wa_raw", [P, 2 * K], U8)
+        wb_raw = tile("wb_raw", [P, K], I32)
+        gs_sb = tile("gs_sb", [P, PACK, T], F32)
+        zs_sb = tile("zs_sb", [P, PACK, T], F32)
+
+        def g_rows(z):
+            return g[z * P * PACK : (z + 1) * P * PACK, :].rearrange("(p j) t -> p j t", j=PACK)
+
+        def load_ab_scales(scales, row):
+            for q in range(4):
+                nc.sync.dma_start(
+                    out=ab_scale_raw[32 * q + row : 32 * q + row + 4, :].bitcast(I32),
+                    in_=scales[0].bitcast(I32)[4 * q : 4 * q + 4, :],
+                )
+
+        nc.sync.dma_start(out=g_raw[0][:], in_=g_rows(0))
+        for q in range(4):
+            nc.sync.dma_start(
+                out=wd_scale_raw[32 * q : 32 * q + 4, :, :].bitcast(I32),
+                in_=wd_scales.bitcast(I32)[:, 4 * q : 4 * q + 4, :].rearrange("z r c -> r z c"),
+            )
+        nc.sync.dma_start(out=wd_raw[:], in_=wd_words.rearrange("z p c r -> p z (c r)").bitcast(I32))
+        nc.sync.dma_start(out=g_raw[1][:], in_=g_rows(1))
+        nc.sync.dma_start(out=wa_raw[:].bitcast(I32), in_=wa_words[0].bitcast(I32))
+        load_ab_scales(wa_scales, 0)
+        gs_rows = gs.rearrange("(p j) t -> p j t", j=PACK)
+        nc.sync.dma_start(out=gs_sb[:, 0:2, :], in_=gs_rows[:, 0:2, :])
+        nc.sync.dma_start(out=gs_sb[:, 2:4, :], in_=gs_rows[:, 2:4, :])
+        load_ab_scales(wb_scales, WB_ROW)
+        nc.sync.dma_start(out=zs_sb[:], in_=zs.rearrange("(p j) t -> p j t", j=PACK))
+        nc.sync.dma_start(out=wb_raw[:], in_=wb_words[0].rearrange("p c r -> p (c r)").bitcast(I32))
+
+        wd_scale = tile("wd_scale", [P, passes, R], U8)
+        wd_codes = tile("wd_codes", [P, passes, R], I32)
+        wa_codes = tile("wa_codes", [P, 2 * K], U8)
+        wb_codes = tile("wb_codes", [P, K], I32)
+        ab_scale = tile("ab_scale", [P, K], U8)
+
+
+        g_codes = [tile("g_codes%d" % z, [P, T], I32) for z in range(passes)]
+        g_scale = [tile("g_scale%d" % z, [P, T], U8) for z in range(passes)]
+
+        def quantize_g(z, between):
+            a = tile("g_a%d" % z, [P, HALF, PACK], BF16)
+            b = tile("g_b%d" % z, [P, HALF, PACK], BF16)
+            nc.scalar.copy(out=word_view(b, 2), in_=rows_view(g_raw[z], HALF, HALF, 2))
+            for u in range(2):
+                nc.vector.tensor_copy(
+                    out=word_view(a[:, u * QUARTER : (u + 1) * QUARTER, :], 2),
+                    in_=rows_view(g_raw[z], u * QUARTER, QUARTER, 2),
+                )
+            between()
+            for u in range(2):
+                quantize(g_codes[z], g_scale[z], u * QUARTER, a[:, u * QUARTER : (u + 1) * QUARTER, :], E5M2)
+            quantize(g_codes[z], g_scale[z], HALF, b, E5M2)
+
+        d_bank = [ps.tile([P, T], F32, name="d_bank%d" % j) for j in range(PACK)]
+        x_bank = [ps.tile([P, T], F32, name="x_bank%d" % j) for j in range(PACK)]
+
+        def d_pass(z):
+            for j in range(PACK):
+                cols = slice(P * j, P * (j + 1))
+                nc.tensor.matmul_mx(
+                    out=d_bank[j][:],
+                    lhsT=wd_codes[:, z, cols].bitcast(E4M3),
+                    lhsT_scale=wd_scale[:, z, cols],
+                    rhs=g_codes[z][:].bitcast(E5M2),
+                    rhs_scale=g_scale[z][:],
+                    start=(z == 0),
+                    stop=(z == passes - 1),
+                )
+
+        def deal_wd_scales():
+            nc.vector.tensor_copy(
+                out=wd_scale[:].rearrange("p z (j a i) -> p z a j i", j=PACK, i=16),
+                in_=wd_scale_raw[:].rearrange("p z (a i j) -> p z a j i", j=PACK, i=16),
+            )
+
+        quantize_g(0, deal_wd_scales)
+        nc.vector.tensor_copy(
+            out=wd_codes[:].rearrange("p z (j a i) -> p z a j i", j=PACK, i=4),
+            in_=wd_raw[:].rearrange("p z (a i j) -> p z a j i", j=PACK, i=4),
+        )
+        d_pass(0)
+        quantize_g(1, lambda: None)
+        d_pass(1)
+        nc.vector.tensor_copy(
+            out=wa_codes[:].rearrange("p (j a i b) -> p a j i b", j=PACK, i=8, b=2),
+            in_=wa_raw[:].rearrange("p (a i j b) -> p a j i b", j=PACK, i=8, b=2),
+        )
+
+        da_rows = tile("da_rows", [P, PACK, HALF], BF16)
+        d_lo = tile("d_lo", [P, PACK, HALF], F32)
+        d_hi = tile("d_hi", [P, PACK, HALF], F32)
+        for j in range(PACK):
+            nc.vector.tensor_tensor(out=da_rows[:, j, :], in0=d_bank[j][:, 0:HALF], in1=gs_sb[:, j, 0:HALF], op=MULT)
+            nc.scalar.copy(out=d_hi[:, j, :], in_=d_bank[j][:, HALF:T])
+        nc.vector.tensor_copy(
+            out=ab_scale[:].rearrange("p (j a i) -> p a j i", j=PACK, i=16),
+            in_=ab_scale_raw[:].rearrange("p (a i j) -> p a j i", j=PACK, i=16),
+        )
+        for j in range(PACK):
+            nc.tensor.matmul_mx(
+                out=x_bank[j][:],
+                lhsT=wa_codes[:, 2 * P * j : 2 * P * (j + 1)].bitcast(E2M1),
+                lhsT_scale=ab_scale[:, P * j : P * (j + 1)],
+                rhs=g_codes[0][:].bitcast(E5M2),
+                rhs_scale=g_scale[0][:],
+                start=True,
+                stop=True,
+            )
+        da_lo = tile("da_lo", [P, HALF, PACK], BF16)
+        da_hi = tile("da_hi", [P, HALF, PACK], BF16)
+        nc.scalar.copy(out=word_view(da_lo, 4), in_=rows_view(da_rows, 0, HALF, 4))
+        nc.vector.tensor_tensor(
+            out=word_view(da_hi, 2), in0=rows_view(d_hi, 0, HALF, 2), in1=rows_view(gs_sb, HALF, HALF, 2), op=MULT
+        )
+        for j in range(PACK):
+            nc.scalar.copy(out=d_lo[:, j, :], in_=d_bank[j][:, 0:HALF])
+        da_codes = tile("da_codes", [P, T], I32)
+        da_scale = tile("da_scale", [P, T], U8)
+        quantize(da_codes, da_scale, 0, da_lo, E5M2)
+        quantize(da_codes, da_scale, HALF, da_hi, E5M2)
+
+        def wa_pass(bank, j):
+            nc.tensor.matmul_mx(
+                out=bank[j][:],
+                lhsT=wa_codes[:, 2 * P * j : 2 * P * (j + 1)].bitcast(E2M1),
+                lhsT_scale=ab_scale[:, P * j : P * (j + 1)],
+                rhs=da_codes[:].bitcast(E5M2),
+                rhs_scale=da_scale[:],
+                start=True,
+                stop=False,
+            )
+
+        db_codes = [tile("db_codes%d" % u, [P, QUARTER], I32) for u in range(4)]
+        db_scale = [tile("db_scale%d" % u, [P, QUARTER], U8) for u in range(4)]
+        db_words = [tile("db_words%d" % u, [P, QUARTER, PACK], BF16) for u in range(4)]
+
+        def db_mul(u):
+            d_half = d_hi if u >= 2 else d_lo
+            nc.vector.tensor_tensor(
+                out=word_view(db_words[u], 2),
+                in0=rows_view(d_half, (u % 2) * QUARTER, QUARTER, 2),
+                in1=rows_view(zs_sb, u * QUARTER, QUARTER, 2),
+                op=MULT,
+            )
+
+        def db_quant(u):
+            quantize(db_codes[u], db_scale[u], 0, db_words[u], E4M3)
+
+        def wb_pass(bank, j, u, stop):
+            nc.tensor.matmul_mx(
+                out=bank[j][:, u * QUARTER : (u + 1) * QUARTER],
+                lhsT=wb_codes[:, P * j : P * (j + 1)].bitcast(E4M3),
+                lhsT_scale=ab_scale[WB_ROW:P, P * j : P * (j + 1)],
+                rhs=db_codes[u][:].bitcast(E4M3),
+                rhs_scale=db_scale[u][:],
+                start=False,
+                stop=stop,
+            )
+
+        for j in range(PACK):
+            wa_pass(x_bank, j)
+        wa_pass(d_bank, 0)
+        db_mul(2)
+        db_mul(3)
+        nc.vector.tensor_copy(
+            out=wb_codes[:].rearrange("p (j a i) -> p a j i", j=PACK, i=4),
+            in_=wb_raw[:].rearrange("p (a i j) -> p a j i", j=PACK, i=4),
+        )
+        db_quant(2)
+        db_quant(3)
+        for j in range(PACK):
+            wb_pass(x_bank, j, 2, False)
+        for j in range(PACK):
+            wb_pass(x_bank, j, 3, True)
+        for j in range(1, PACK):
+            wa_pass(d_bank, j)
+        db_mul(0)
+        db_mul(1)
+        db_quant(0)
+        db_quant(1)
+        for j in range(PACK):
+            wb_pass(d_bank, j, 0, False)
+        for j in range(PACK):
+            wb_pass(d_bank, j, 1, True)
+
+        y_rows = out_0.rearrange("(p j) t -> p j t", j=PACK)
+        y_words_out = out_1[0].rearrange("p c r -> p (c r)").bitcast(I32)
+        y_hi = tile("y_hi", [P, PACK, HALF], F32)
+        y_lo = tile("y_lo", [P, PACK, HALF], F32)
+        y_codes = tile("y_codes", [P, T], I32)
+        y_scale = tile("y_scale", [P, T], U8)
+        for j in range(PACK):
+            nc.scalar.copy(out=y_hi[:, j, :], in_=x_bank[j][:, HALF:T])
+        nc.sync.dma_start(out=y_rows[:, :, HALF:T], in_=y_hi[:])
+        yw_hi = tile("yw_hi", [P, HALF, PACK], BF16)
+        nc.vector.tensor_copy(out=word_view(yw_hi, 2), in_=rows_view(y_hi, 0, HALF, 2))
+        for j in range(PACK - 1):
+            nc.scalar.copy(out=y_lo[:, j, :], in_=d_bank[j][:, 0:HALF])
+            if j == 1:
+                nc.sync.dma_start(out=y_rows[:, 0:2, 0:HALF], in_=y_lo[:, 0:2, :])
+        nc.vector.tensor_copy(out=y_lo[:, 3, :], in_=d_bank[3][:, 0:HALF])
+        nc.sync.dma_start(out=y_rows[:, 2:4, 0:HALF], in_=y_lo[:, 2:4, :])
+        quantize(y_codes, y_scale, HALF, yw_hi, E4M3)
+        nc.sync.dma_start(out=y_words_out[:, HALF:T], in_=y_codes[:, HALF:T])
+        yw_0 = tile("yw_0", [P, QUARTER, PACK], BF16)
+        yw_1 = tile("yw_1", [P, QUARTER, PACK], BF16)
+        nc.vector.tensor_copy(out=word_view(yw_0, 2), in_=rows_view(y_lo, 0, QUARTER, 2))
+        nc.scalar.copy(out=word_view(yw_1, 2), in_=rows_view(y_lo, QUARTER, QUARTER, 2))
+        quantize(y_codes, y_scale, 0, yw_0, E4M3)
+        quantize(y_codes, y_scale, QUARTER, yw_1, E4M3)
+        nc.sync.dma_start(out=y_words_out[:, 0:HALF], in_=y_codes[:, 0:HALF])
+        for q in range(4):
+            engine = nc.scalar if q < 2 else nc.sync
+            engine.dma_start(
+                out=out_2[0].bitcast(I32)[4 * q : 4 * q + 4, :],
+                in_=y_scale[32 * q : 32 * q + 4, :].bitcast(I32),
+            )

@@ -18,6 +18,7 @@ P = 128
 PACK = 4
 HALF = T // 2
 QUARTER = T // 4
+EIGHTH = T // 8
 WB_ROW = 4
 
 
@@ -54,39 +55,44 @@ def tile_mix_gradient_of_gated_sum_pl_kernel(
         nc.vector.memset(wd_scale_raw[:].bitcast(I32), 0)
         nc.gpsimd.memset(ab_scale_raw[:].bitcast(I32), 0)
 
-        g_raw = [tile("g_raw%d" % z, [P, PACK, T], F32) for z in range(passes)]
+        g0_raw = tile("g0_raw", [P, PACK, T], F32)
+        g1_raw = [tile("g1_raw%d" % h, [P, PACK, HALF], F32) for h in range(2)]
         wd_raw = tile("wd_raw", [P, passes, R], I32)
         wa_raw = tile("wa_raw", [P, 2 * K], U8)
         wb_raw = tile("wb_raw", [P, K], I32)
-        gs_sb = tile("gs_sb", [P, PACK, T], F32)
-        zs_sb = tile("zs_sb", [P, PACK, T], F32)
+        gs_sb = [tile("gs_sb%d" % h, [P, PACK, HALF], F32) for h in range(2)]
+        zs_sb = [tile("zs_sb%d" % h, [P, PACK, HALF], F32) for h in range(2)]
 
-        def g_rows(z):
-            return g[z * P * PACK : (z + 1) * P * PACK, :].rearrange("(p j) t -> p j t", j=PACK)
+        def by_word(rows):
+            return rows.rearrange("(p j) t -> p j t", j=PACK)
 
-        def load_ab_scales(scales, row):
-            for q in range(4):
-                nc.sync.dma_start(
-                    out=ab_scale_raw[32 * q + row : 32 * q + row + 4, :].bitcast(I32),
-                    in_=scales[0].bitcast(I32)[4 * q : 4 * q + 4, :],
+        def load_half(dst, rows, h):
+            nc.sync.dma_start(out=dst[h][:], in_=by_word(rows)[:, :, h * HALF : (h + 1) * HALF])
+
+        def load_ab_scales(engine, scales, row):
+            for r in range(4):
+                engine.dma_start(
+                    out=ab_scale_raw[row + r : P : 32, :].bitcast(I32),
+                    in_=scales[0].bitcast(I32)[r:16:4, :],
                 )
 
-        nc.sync.dma_start(out=g_raw[0][:], in_=g_rows(0))
-        for q in range(4):
+        load_ab_scales(nc.gpsimd, wa_scales, 0)
+        nc.sync.dma_start(out=g0_raw[:], in_=by_word(g[0 : P * PACK, :]))
+        for r in range(4):
             nc.sync.dma_start(
-                out=wd_scale_raw[32 * q : 32 * q + 4, :, :].bitcast(I32),
-                in_=wd_scales.bitcast(I32)[:, 4 * q : 4 * q + 4, :].rearrange("z r c -> r z c"),
+                out=wd_scale_raw[r:P:32, :, :].bitcast(I32),
+                in_=wd_scales.bitcast(I32)[:, r:16:4, :].rearrange("z q c -> q z c"),
             )
         nc.sync.dma_start(out=wd_raw[:], in_=wd_words.rearrange("z p c r -> p z (c r)").bitcast(I32))
-        nc.sync.dma_start(out=g_raw[1][:], in_=g_rows(1))
+        load_half(g1_raw, g[P * PACK : N, :], 0)
+        load_half(g1_raw, g[P * PACK : N, :], 1)
         nc.sync.dma_start(out=wa_raw[:].bitcast(I32), in_=wa_words[0].bitcast(I32))
-        load_ab_scales(wa_scales, 0)
-        gs_rows = gs.rearrange("(p j) t -> p j t", j=PACK)
-        nc.sync.dma_start(out=gs_sb[:, 0:2, :], in_=gs_rows[:, 0:2, :])
-        nc.sync.dma_start(out=gs_sb[:, 2:4, :], in_=gs_rows[:, 2:4, :])
-        load_ab_scales(wb_scales, WB_ROW)
-        nc.sync.dma_start(out=zs_sb[:], in_=zs.rearrange("(p j) t -> p j t", j=PACK))
+        load_half(gs_sb, gs, 0)
+        load_ab_scales(nc.sync, wb_scales, WB_ROW)
         nc.sync.dma_start(out=wb_raw[:], in_=wb_words[0].rearrange("p c r -> p (c r)").bitcast(I32))
+        load_half(gs_sb, gs, 1)
+        load_half(zs_sb, zs, 1)
+        load_half(zs_sb, zs, 0)
 
         wd_scale = tile("wd_scale", [P, passes, R], U8)
         wd_codes = tile("wd_codes", [P, passes, R], I32)
@@ -98,19 +104,13 @@ def tile_mix_gradient_of_gated_sum_pl_kernel(
         g_codes = [tile("g_codes%d" % z, [P, T], I32) for z in range(passes)]
         g_scale = [tile("g_scale%d" % z, [P, T], U8) for z in range(passes)]
 
-        def quantize_g(z, between):
-            a = tile("g_a%d" % z, [P, HALF, PACK], BF16)
-            b = tile("g_b%d" % z, [P, HALF, PACK], BF16)
-            nc.scalar.copy(out=word_view(b, 2), in_=rows_view(g_raw[z], HALF, HALF, 2))
-            for u in range(2):
-                nc.vector.tensor_copy(
-                    out=word_view(a[:, u * QUARTER : (u + 1) * QUARTER, :], 2),
-                    in_=rows_view(g_raw[z], u * QUARTER, QUARTER, 2),
-                )
-            between()
-            for u in range(2):
-                quantize(g_codes[z], g_scale[z], u * QUARTER, a[:, u * QUARTER : (u + 1) * QUARTER, :], E5M2)
-            quantize(g_codes[z], g_scale[z], HALF, b, E5M2)
+        def round_g(engine_copy, name, raw, t0, width):
+            grouped = tile(name, [P, width, PACK], BF16)
+            engine_copy(out=word_view(grouped, 2), in_=rows_view(raw, t0, width, 2))
+            return grouped
+
+        def quantize_g(z, t0, grouped):
+            quantize(g_codes[z], g_scale[z], t0, grouped, E5M2)
 
         d_bank = [ps.tile([P, T], F32, name="d_bank%d" % j) for j in range(PACK)]
         x_bank = [ps.tile([P, T], F32, name="x_bank%d" % j) for j in range(PACK)]
@@ -128,19 +128,39 @@ def tile_mix_gradient_of_gated_sum_pl_kernel(
                     stop=(z == passes - 1),
                 )
 
-        def deal_wd_scales():
-            nc.vector.tensor_copy(
-                out=wd_scale[:].rearrange("p z (j a i) -> p z a j i", j=PACK, i=16),
-                in_=wd_scale_raw[:].rearrange("p z (a i j) -> p z a j i", j=PACK, i=16),
-            )
-
-        quantize_g(0, deal_wd_scales)
+        g0_hi = round_g(nc.scalar.copy, "g0_hi", g0_raw, HALF, HALF)
+        g0_lo = round_g(nc.vector.tensor_copy, "g0_lo", g0_raw, 0, HALF)
+        nc.vector.tensor_copy(
+            out=wd_scale[:].rearrange("p z (j a i) -> p z a j i", j=PACK, i=16),
+            in_=wd_scale_raw[:].rearrange("p z (a i j) -> p z a j i", j=PACK, i=16),
+        )
+        quantize_g(0, 0, g0_lo)
         nc.vector.tensor_copy(
             out=wd_codes[:].rearrange("p z (j a i) -> p z a j i", j=PACK, i=4),
             in_=wd_raw[:].rearrange("p z (a i j) -> p z a j i", j=PACK, i=4),
         )
+        quantize_g(0, HALF, g0_hi)
+        for j in range(3):
+            nc.tensor.matmul_mx(
+                out=x_bank[j][:],
+                lhsT=wd_raw[:, 0, 0:P].bitcast(E4M3),
+                lhsT_scale=wd_scale_raw[:, 0, 0:P],
+                rhs=wd_raw[:, 1, :].bitcast(E4M3),
+                rhs_scale=wd_scale_raw[:, 1, :],
+                start=True,
+                stop=True,
+            )
         d_pass(0)
-        quantize_g(1, lambda: None)
+        g1_b = round_g(nc.scalar.copy, "g1_b", g1_raw[0], QUARTER, QUARTER)
+        g1_a = round_g(nc.vector.tensor_copy, "g1_a", g1_raw[0], 0, QUARTER)
+        quantize_g(1, 0, g1_a)
+        quantize_g(1, QUARTER, g1_b)
+        g1_e = round_g(nc.scalar.copy, "g1_e", g1_raw[1], QUARTER + EIGHTH, EIGHTH)
+        g1_c = round_g(nc.vector.tensor_copy, "g1_c", g1_raw[1], 0, QUARTER)
+        g1_d = round_g(nc.vector.tensor_copy, "g1_d", g1_raw[1], QUARTER, EIGHTH)
+        quantize_g(1, HALF, g1_c)
+        quantize_g(1, HALF + QUARTER + EIGHTH, g1_e)
+        quantize_g(1, HALF + QUARTER, g1_d)
         d_pass(1)
         nc.vector.tensor_copy(
             out=wa_codes[:].rearrange("p (j a i b) -> p a j i b", j=PACK, i=8, b=2),
@@ -151,13 +171,18 @@ def tile_mix_gradient_of_gated_sum_pl_kernel(
         d_lo = tile("d_lo", [P, PACK, HALF], F32)
         d_hi = tile("d_hi", [P, PACK, HALF], F32)
         for j in range(PACK):
-            nc.vector.tensor_tensor(out=da_rows[:, j, :], in0=d_bank[j][:, 0:HALF], in1=gs_sb[:, j, 0:HALF], op=MULT)
+            nc.vector.tensor_tensor(out=da_rows[:, j, :], in0=d_bank[j][:, 0:HALF], in1=gs_sb[0][:, j, :], op=MULT)
             nc.scalar.copy(out=d_hi[:, j, :], in_=d_bank[j][:, HALF:T])
         nc.vector.tensor_copy(
             out=ab_scale[:].rearrange("p (j a i) -> p a j i", j=PACK, i=16),
             in_=ab_scale_raw[:].rearrange("p (a i j) -> p a j i", j=PACK, i=16),
         )
-        for j in range(PACK):
+        nc.vector.tensor_copy(
+            out=wb_codes[:].rearrange("p (j a i) -> p a j i", j=PACK, i=4),
+            in_=wb_raw[:].rearrange("p (a i j) -> p a j i", j=PACK, i=4),
+        )
+        for n in range(5):
+            j = n % PACK
             nc.tensor.matmul_mx(
                 out=x_bank[j][:],
                 lhsT=wa_codes[:, 2 * P * j : 2 * P * (j + 1)].bitcast(E2M1),
@@ -171,7 +196,7 @@ def tile_mix_gradient_of_gated_sum_pl_kernel(
         da_hi = tile("da_hi", [P, HALF, PACK], BF16)
         nc.scalar.copy(out=word_view(da_lo, 4), in_=rows_view(da_rows, 0, HALF, 4))
         nc.vector.tensor_tensor(
-            out=word_view(da_hi, 2), in0=rows_view(d_hi, 0, HALF, 2), in1=rows_view(gs_sb, HALF, HALF, 2), op=MULT
+            out=word_view(da_hi, 2), in0=rows_view(d_hi, 0, HALF, 2), in1=rows_view(gs_sb[1], 0, HALF, 2), op=MULT
         )
         for j in range(PACK):
             nc.scalar.copy(out=d_lo[:, j, :], in_=d_bank[j][:, 0:HALF])
@@ -200,7 +225,7 @@ def tile_mix_gradient_of_gated_sum_pl_kernel(
             nc.vector.tensor_tensor(
                 out=word_view(db_words[u], 2),
                 in0=rows_view(d_half, (u % 2) * QUARTER, QUARTER, 2),
-                in1=rows_view(zs_sb, u * QUARTER, QUARTER, 2),
+                in1=rows_view(zs_sb[u // 2], (u % 2) * QUARTER, QUARTER, 2),
                 op=MULT,
             )
 
@@ -223,15 +248,10 @@ def tile_mix_gradient_of_gated_sum_pl_kernel(
         wa_pass(d_bank, 0)
         db_mul(2)
         db_mul(3)
-        nc.vector.tensor_copy(
-            out=wb_codes[:].rearrange("p (j a i) -> p a j i", j=PACK, i=4),
-            in_=wb_raw[:].rearrange("p (a i j) -> p a j i", j=PACK, i=4),
-        )
         db_quant(2)
         db_quant(3)
         for j in range(PACK):
             wb_pass(x_bank, j, 2, False)
-        for j in range(PACK):
             wb_pass(x_bank, j, 3, True)
         for j in range(1, PACK):
             wa_pass(d_bank, j)
@@ -241,7 +261,6 @@ def tile_mix_gradient_of_gated_sum_pl_kernel(
         db_quant(1)
         for j in range(PACK):
             wb_pass(d_bank, j, 0, False)
-        for j in range(PACK):
             wb_pass(d_bank, j, 1, True)
 
         y_rows = out_0.rearrange("(p j) t -> p j t", j=PACK)
@@ -252,7 +271,8 @@ def tile_mix_gradient_of_gated_sum_pl_kernel(
         y_scale = tile("y_scale", [P, T], U8)
         for j in range(PACK):
             nc.scalar.copy(out=y_hi[:, j, :], in_=x_bank[j][:, HALF:T])
-        nc.sync.dma_start(out=y_rows[:, :, HALF:T], in_=y_hi[:])
+            if j % 2 == 1:
+                nc.sync.dma_start(out=y_rows[:, j - 1 : j + 1, HALF:T], in_=y_hi[:, j - 1 : j + 1, :])
         yw_hi = tile("yw_hi", [P, HALF, PACK], BF16)
         nc.vector.tensor_copy(out=word_view(yw_hi, 2), in_=rows_view(y_hi, 0, HALF, 2))
         for j in range(PACK - 1):
@@ -264,14 +284,17 @@ def tile_mix_gradient_of_gated_sum_pl_kernel(
         quantize(y_codes, y_scale, HALF, yw_hi, E4M3)
         nc.sync.dma_start(out=y_words_out[:, HALF:T], in_=y_codes[:, HALF:T])
         yw_0 = tile("yw_0", [P, QUARTER, PACK], BF16)
-        yw_1 = tile("yw_1", [P, QUARTER, PACK], BF16)
+        yw_1 = tile("yw_1", [P, EIGHTH, PACK], BF16)
+        yw_2 = tile("yw_2", [P, EIGHTH, PACK], BF16)
         nc.vector.tensor_copy(out=word_view(yw_0, 2), in_=rows_view(y_lo, 0, QUARTER, 2))
-        nc.scalar.copy(out=word_view(yw_1, 2), in_=rows_view(y_lo, QUARTER, QUARTER, 2))
+        nc.vector.tensor_copy(out=word_view(yw_1, 2), in_=rows_view(y_lo, QUARTER, EIGHTH, 2))
+        nc.scalar.copy(out=word_view(yw_2, 2), in_=rows_view(y_lo, QUARTER + EIGHTH, EIGHTH, 2))
         quantize(y_codes, y_scale, 0, yw_0, E4M3)
+        quantize(y_codes, y_scale, QUARTER + EIGHTH, yw_2, E4M3)
         quantize(y_codes, y_scale, QUARTER, yw_1, E4M3)
         nc.sync.dma_start(out=y_words_out[:, 0:HALF], in_=y_codes[:, 0:HALF])
         for q in range(4):
-            engine = nc.scalar if q < 2 else nc.sync
+            engine = nc.scalar if q < 3 else nc.sync
             engine.dma_start(
                 out=out_2[0].bitcast(I32)[4 * q : 4 * q + 4, :],
                 in_=y_scale[32 * q : 32 * q + 4, :].bitcast(I32),

from contextlib import ExitStack

import concourse.mybir as mybir

N, R, K, T = 1024, 512, 512, 512
FLOPS = 2 * T * (N * R + 2 * R * K)

F32 = mybir.dt.float32
BF16 = mybir.dt.bfloat16
I32 = mybir.dt.int32
U8 = mybir.dt.uint8
E4M3 = mybir.dt.float8_e4m3fn_x4
E5M2 = mybir.dt.float8_e5m2_x4
E2M1 = mybir.dt.float4_e2m1fn_x4
MULT = mybir.AluOpType.mult

P = 128
PACK = 4
HALF = T // 2
QUARTER = T // 4
EIGHTH = T // 8
WB_ROW = 4


def tile_mix_gradient_of_gated_sum_pl_kernel(
    tc, g, wd_words, wd_scales, gs, zs, wa_words, wa_scales, wb_words, wb_scales, out_0, out_1, out_2
):
    nc = tc.nc
    passes = N // (P * PACK)

    with ExitStack() as ctx:
        sb = ctx.enter_context(tc.tile_pool(name="sb", bufs=1))
        ps = ctx.enter_context(tc.psum_pool(name="ps", bufs=1))
        ctx.enter_context(tc.manual_schedule())

        def tile(name, shape, dtype):
            return sb.tile(shape, dtype, name=name, align_bytes=64)

        def rows_view(src, t0, width, run):
            return src[:, :, t0 : t0 + width].rearrange("p j (c i) -> p c j i", i=run)

        def word_view(dst, run):
            return dst[:].rearrange("p (c i) j -> p c j i", i=run)

        def quantize(codes, scales, t0, grouped, fmt):
            width = grouped.shape[1]
            nc.vector.quantize_mx(
                out=codes[:, t0 : t0 + width].bitcast(fmt),
                scales=scales[:, t0 : t0 + width],
                in_=grouped[:].rearrange("p t j -> p (t j)"),
            )

        wd_scale_raw = tile("wd_scale_raw", [P, passes, R], U8)
        ab_scale_raw = tile("ab_scale_raw", [P, K], U8)
        nc.vector.memset(wd_scale_raw[:].bitcast(I32), 0)
        nc.gpsimd.memset(ab_scale_raw[:].bitcast(I32), 0)

        g0_raw = tile("g0_raw", [P, PACK, T], F32)
        g1_raw = [tile("g1_raw%d" % h, [P, PACK, HALF], F32) for h in range(2)]
        wd_raw = tile("wd_raw", [P, passes, R], I32)
        wa_raw = tile("wa_raw", [P, 2 * K], U8)
        wb_raw = tile("wb_raw", [P, K], I32)
        gs_sb = [tile("gs_sb%d" % h, [P, PACK, HALF], F32) for h in range(2)]
        zs_sb = [tile("zs_sb%d" % h, [P, PACK, HALF], F32) for h in range(2)]

        def by_word(rows):
            return rows.rearrange("(p j) t -> p j t", j=PACK)

        def load_half(dst, rows, h):
            nc.sync.dma_start(out=dst[h][:], in_=by_word(rows)[:, :, h * HALF : (h + 1) * HALF])

        def load_ab_scales(engine, scales, row):
            for r in range(4):
                engine.dma_start(
                    out=ab_scale_raw[row + r : P : 32, :].bitcast(I32),
                    in_=scales[0].bitcast(I32)[r:16:4, :],
                )

        load_ab_scales(nc.gpsimd, wa_scales, 0)
        nc.sync.dma_start(out=g0_raw[:], in_=by_word(g[0 : P * PACK, :]))
        for r in range(4):
            nc.sync.dma_start(
                out=wd_scale_raw[r:P:32, :, :].bitcast(I32),
                in_=wd_scales.bitcast(I32)[:, r:16:4, :].rearrange("z q c -> q z c"),
            )
        nc.sync.dma_start(out=wd_raw[:], in_=wd_words.rearrange("z p c r -> p z (c r)").bitcast(I32))
        load_half(g1_raw, g[P * PACK : N, :], 0)
        load_half(g1_raw, g[P * PACK : N, :], 1)
        nc.sync.dma_start(out=wa_raw[:].bitcast(I32), in_=wa_words[0].bitcast(I32))
        load_half(gs_sb, gs, 0)
        load_ab_scales(nc.sync, wb_scales, WB_ROW)
        nc.sync.dma_start(out=wb_raw[:], in_=wb_words[0].rearrange("p c r -> p (c r)").bitcast(I32))
        load_half(gs_sb, gs, 1)
        load_half(zs_sb, zs, 1)
        load_half(zs_sb, zs, 0)

        wd_scale = tile("wd_scale", [P, passes, R], U8)
        wd_codes = tile("wd_codes", [P, passes, R], I32)
        wa_codes = tile("wa_codes", [P, 2 * K], U8)
        wb_codes = tile("wb_codes", [P, K], I32)
        ab_scale = tile("ab_scale", [P, K], U8)


        g_codes = [tile("g_codes%d" % z, [P, T], I32) for z in range(passes)]
        g_scale = [tile("g_scale%d" % z, [P, T], U8) for z in range(passes)]

        def round_g(engine_copy, name, raw, t0, width):
            grouped = tile(name, [P, width, PACK], BF16)
            engine_copy(out=word_view(grouped, 2), in_=rows_view(raw, t0, width, 2))
            return grouped

        def quantize_g(z, t0, grouped):
            quantize(g_codes[z], g_scale[z], t0, grouped, E5M2)

        d_bank = [ps.tile([P, T], F32, name="d_bank%d" % j) for j in range(PACK)]
        x_bank = [ps.tile([P, T], F32, name="x_bank%d" % j) for j in range(PACK)]

        def d_pass(z):
            for j in range(PACK):
                cols = slice(P * j, P * (j + 1))
                nc.tensor.matmul_mx(
                    out=d_bank[j][:],
                    lhsT=wd_codes[:, z, cols].bitcast(E4M3),
                    lhsT_scale=wd_scale[:, z, cols],
                    rhs=g_codes[z][:].bitcast(E5M2),
                    rhs_scale=g_scale[z][:],
                    start=(z == 0),
                    stop=(z == passes - 1),
                )

        g0_hi = round_g(nc.scalar.copy, "g0_hi", g0_raw, HALF, HALF)
        g0_lo = round_g(nc.vector.tensor_copy, "g0_lo", g0_raw, 0, HALF)
        nc.vector.tensor_copy(
            out=wd_scale[:].rearrange("p z (j a i) -> p z a j i", j=PACK, i=16),
            in_=wd_scale_raw[:].rearrange("p z (a i j) -> p z a j i", j=PACK, i=16),
        )
        quantize_g(0, 0, g0_lo)
        nc.vector.tensor_copy(
            out=wd_codes[:].rearrange("p z (j a i) -> p z a j i", j=PACK, i=4),
            in_=wd_raw[:].rearrange("p z (a i j) -> p z a j i", j=PACK, i=4),
        )
        quantize_g(0, HALF, g0_hi)
        for j in range(3):
            nc.tensor.matmul_mx(
                out=x_bank[j][:],
                lhsT=wd_raw[:, 0, 0:P].bitcast(E4M3),
                lhsT_scale=wd_scale_raw[:, 0, 0:P],
                rhs=wd_raw[:, 1, :].bitcast(E4M3),
                rhs_scale=wd_scale_raw[:, 1, :],
                start=True,
                stop=True,
            )
        d_pass(0)
        g1_b = round_g(nc.scalar.copy, "g1_b", g1_raw[0], QUARTER, QUARTER)
        g1_a = round_g(nc.vector.tensor_copy, "g1_a", g1_raw[0], 0, QUARTER)
        quantize_g(1, 0, g1_a)
        quantize_g(1, QUARTER, g1_b)
        g1_e = round_g(nc.scalar.copy, "g1_e", g1_raw[1], QUARTER + EIGHTH, EIGHTH)
        g1_c = round_g(nc.vector.tensor_copy, "g1_c", g1_raw[1], 0, QUARTER)
        g1_d = round_g(nc.vector.tensor_copy, "g1_d", g1_raw[1], QUARTER, EIGHTH)
        quantize_g(1, HALF, g1_c)
        quantize_g(1, HALF + QUARTER + EIGHTH, g1_e)
        quantize_g(1, HALF + QUARTER, g1_d)
        d_pass(1)
        nc.vector.tensor_copy(
            out=wa_codes[:].rearrange("p (j a i b) -> p a j i b", j=PACK, i=8, b=2),
            in_=wa_raw[:].rearrange("p (a i j b) -> p a j i b", j=PACK, i=8, b=2),
        )

        da_rows = tile("da_rows", [P, PACK, HALF], BF16)
        d_lo = tile("d_lo", [P, PACK, HALF], F32)
        d_hi = tile("d_hi", [P, PACK, HALF], F32)
        for j in range(PACK):
            nc.vector.tensor_tensor(out=da_rows[:, j, :], in0=d_bank[j][:, 0:HALF], in1=gs_sb[0][:, j, :], op=MULT)
            nc.scalar.copy(out=d_hi[:, j, :], in_=d_bank[j][:, HALF:T])
        nc.vector.tensor_copy(
            out=ab_scale[:].rearrange("p (j a i) -> p a j i", j=PACK, i=16),
            in_=ab_scale_raw[:].rearrange("p (a i j) -> p a j i", j=PACK, i=16),
        )
        nc.vector.tensor_copy(
            out=wb_codes[:].rearrange("p (j a i) -> p a j i", j=PACK, i=4),
            in_=wb_raw[:].rearrange("p (a i j) -> p a j i", j=PACK, i=4),
        )
        for n in range(5):
            j = n % PACK
            nc.tensor.matmul_mx(
                out=x_bank[j][:],
                lhsT=wa_codes[:, 2 * P * j : 2 * P * (j + 1)].bitcast(E2M1),
                lhsT_scale=ab_scale[:, P * j : P * (j + 1)],
                rhs=g_codes[0][:].bitcast(E5M2),
                rhs_scale=g_scale[0][:],
                start=True,
                stop=True,
            )
        da_lo = tile("da_lo", [P, HALF, PACK], BF16)
        da_hi = tile("da_hi", [P, HALF, PACK], BF16)
        nc.scalar.copy(out=word_view(da_lo, 4), in_=rows_view(da_rows, 0, HALF, 4))
        nc.vector.tensor_tensor(
            out=word_view(da_hi, 2), in0=rows_view(d_hi, 0, HALF, 2), in1=rows_view(gs_sb[1], 0, HALF, 2), op=MULT
        )
        for j in range(PACK):
            nc.scalar.copy(out=d_lo[:, j, :], in_=d_bank[j][:, 0:HALF])
        da_codes = tile("da_codes", [P, T], I32)
        da_scale = tile("da_scale", [P, T], U8)
        quantize(da_codes, da_scale, 0, da_lo, E5M2)
        quantize(da_codes, da_scale, HALF, da_hi, E5M2)

        def wa_pass(bank, j):
            nc.tensor.matmul_mx(
                out=bank[j][:],
                lhsT=wa_codes[:, 2 * P * j : 2 * P * (j + 1)].bitcast(E2M1),
                lhsT_scale=ab_scale[:, P * j : P * (j + 1)],
                rhs=da_codes[:].bitcast(E5M2),
                rhs_scale=da_scale[:],
                start=True,
                stop=False,
            )

        db_codes = [tile("db_codes%d" % u, [P, QUARTER], I32) for u in range(4)]
        db_scale = [tile("db_scale%d" % u, [P, QUARTER], U8) for u in range(4)]
        db_words = [tile("db_words%d" % u, [P, QUARTER, PACK], BF16) for u in range(4)]

        def db_mul(u):
            d_half = d_hi if u >= 2 else d_lo
            nc.vector.tensor_tensor(
                out=word_view(db_words[u], 2),
                in0=rows_view(d_half, (u % 2) * QUARTER, QUARTER, 2),
                in1=rows_view(zs_sb[u // 2], (u % 2) * QUARTER, QUARTER, 2),
                op=MULT,
            )

        def db_quant(u):
            quantize(db_codes[u], db_scale[u], 0, db_words[u], E4M3)

        def wb_pass(bank, j, u, stop):
            nc.tensor.matmul_mx(
                out=bank[j][:, u * QUARTER : (u + 1) * QUARTER],
                lhsT=wb_codes[:, P * j : P * (j + 1)].bitcast(E4M3),
                lhsT_scale=ab_scale[WB_ROW:P, P * j : P * (j + 1)],
                rhs=db_codes[u][:].bitcast(E4M3),
                rhs_scale=db_scale[u][:],
                start=False,
                stop=stop,
            )

        for j in range(PACK):
            wa_pass(x_bank, j)
        wa_pass(d_bank, 0)
        db_mul(2)
        db_mul(3)
        db_quant(2)
        db_quant(3)
        for j in range(PACK):
            wb_pass(x_bank, j, 2, False)
            wb_pass(x_bank, j, 3, True)
        for j in range(1, PACK):
            wa_pass(d_bank, j)
        db_mul(0)
        db_mul(1)
        db_quant(0)
        db_quant(1)
        for j in range(PACK):
            wb_pass(d_bank, j, 0, False)
            wb_pass(d_bank, j, 1, True)

        y_rows = out_0.rearrange("(p j) t -> p j t", j=PACK)
        y_words_out = out_1[0].rearrange("p c r -> p (c r)").bitcast(I32)
        y_hi = tile("y_hi", [P, PACK, HALF], F32)
        y_lo = tile("y_lo", [P, PACK, HALF], F32)
        y_codes = tile("y_codes", [P, T], I32)
        y_scale = tile("y_scale", [P, T], U8)
        for j in range(PACK):
            nc.scalar.copy(out=y_hi[:, j, :], in_=x_bank[j][:, HALF:T])
            if j % 2 == 1:
                nc.sync.dma_start(out=y_rows[:, j - 1 : j + 1, HALF:T], in_=y_hi[:, j - 1 : j + 1, :])
        yw_hi = tile("yw_hi", [P, HALF, PACK], BF16)
        nc.vector.tensor_copy(out=word_view(yw_hi, 2), in_=rows_view(y_hi, 0, HALF, 2))
        for j in range(PACK - 1):
            nc.scalar.copy(out=y_lo[:, j, :], in_=d_bank[j][:, 0:HALF])
            if j == 1:
                nc.sync.dma_start(out=y_rows[:, 0:2, 0:HALF], in_=y_lo[:, 0:2, :])
        nc.vector.tensor_copy(out=y_lo[:, 3, :], in_=d_bank[3][:, 0:HALF])
        nc.sync.dma_start(out=y_rows[:, 2:4, 0:HALF], in_=y_lo[:, 2:4, :])
        quantize(y_codes, y_scale, HALF, yw_hi, E4M3)
        nc.sync.dma_start(out=y_words_out[:, HALF:T], in_=y_codes[:, HALF:T])
        yw_0 = tile("yw_0", [P, QUARTER, PACK], BF16)
        yw_1 = tile("yw_1", [P, EIGHTH, PACK], BF16)
        yw_2 = tile("yw_2", [P, EIGHTH, PACK], BF16)
        nc.vector.tensor_copy(out=word_view(yw_0, 2), in_=rows_view(y_lo, 0, QUARTER, 2))
        nc.vector.tensor_copy(out=word_view(yw_1, 2), in_=rows_view(y_lo, QUARTER, EIGHTH, 2))
        nc.scalar.copy(out=word_view(yw_2, 2), in_=rows_view(y_lo, QUARTER + EIGHTH, EIGHTH, 2))
        quantize(y_codes, y_scale, 0, yw_0, E4M3)
        quantize(y_codes, y_scale, QUARTER + EIGHTH, yw_2, E4M3)
        quantize(y_codes, y_scale, QUARTER, yw_1, E4M3)
        nc.sync.dma_start(out=y_words_out[:, 0:HALF], in_=y_codes[:, 0:HALF])
        for q in range(4):
            engine = nc.scalar if q < 3 else nc.sync
            engine.dma_start(
                out=out_2[0].bitcast(I32)[4 * q : 4 * q + 4, :],
                in_=y_scale[32 * q : 32 * q + 4, :].bitcast(I32),
            )
